import numpy as np
import ml_dtypes


def mxq(x, axis, fmt="e4m3"):
    dtype, down = {"e4m3": (ml_dtypes.float8_e4m3fn, 7), "e5m2": (ml_dtypes.float8_e5m2, 14)}[fmt]
    v = np.moveaxis(np.asarray(x, np.float32).astype(ml_dtypes.bfloat16).astype(np.float64), axis, -1)
    blocks = v.reshape(v.shape[:-1] + (-1, 32))
    amax = np.abs(blocks).max(-1, keepdims=True)
    byte = np.maximum(np.where(amax > 0, np.frexp(amax)[1] - 1 + 127, 0) - down, 1)
    scale = np.exp2(byte - 127.0)
    codes = (blocks / scale).astype(np.float32).astype(dtype).astype(np.float64)
    return np.moveaxis((codes * scale).reshape(v.shape), -1, axis)


WIDE = False


def mx_kscale(k):
    if not WIDE:
        return np.ones(k)
    levels = np.array([10, -10, 5, -5, 0])
    if k % 512:
        return np.exp2(np.random.permutation(np.resize(levels, k // 32))).repeat(32)
    a = np.empty((k // 512, 16))
    for p in range(k // 512):
        a[p, :8] = np.random.permutation(np.resize(levels, 8))
        for g in range(8):
            far = levels[np.abs(levels - a[p, g]) >= 10]
            a[p, g + 8] = far[np.random.randint(len(far))]
    return np.exp2(a.ravel()).repeat(32)


def f64(x):
    return np.asarray(x).astype(np.float64)


def striped(idx):
    return np.tile(idx.reshape(-1, 16).T, (8, 1)).astype(np.uint16)


def unstriped(offs):
    return offs[:16].T.reshape(-1).astype(np.int64)


E2M1 = np.array([0.0, 0.5, 1.0, 1.5, 2.0, 3.0, 4.0, 6.0, -0.0, -0.5, -1.0, -1.5, -2.0, -3.0, -4.0, -6.0])


def pack_weight(w, fmt):
    k, n = w.shape
    w = f64(np.asarray(w, np.float32).astype(ml_dtypes.bfloat16)).reshape(k // 32, 32, n)
    amax = np.abs(w).max(1)
    if fmt == "e4m3":
        byte = np.frexp(amax)[1] - 1 + 127 - 7
    else:
        mant, ex = np.frexp(amax / 6.0)
        byte = np.where(mant > 0.5, ex, ex - 1) + 127
    byte = np.clip(np.where(amax > 0, byte, 1), 1, 254)
    scaled = (w * np.exp2(127.0 - byte)[:, None, :]).reshape(k, n).astype(np.float32)
    by_word = np.ascontiguousarray(scaled.reshape(k // 512, 128, 4, n).transpose(0, 1, 3, 2))
    if fmt == "e4m3":
        words = by_word.astype(ml_dtypes.float8_e4m3fn).view(np.uint8)
    else:
        c = by_word.astype(ml_dtypes.float4_e2m1fn).view(np.uint8) & 0xF
        words = (c[..., 0::2] | (c[..., 1::2] << 4)).reshape(k // 512, 128, 2 * n)
    return np.ascontiguousarray(words), np.ascontiguousarray(byte.astype(np.uint8).reshape(k // 512, 16, n))


def unpack_weight(words, scales, fmt):
    g, _, n = scales.shape
    words = np.ascontiguousarray(words).reshape(g, 128, n, -1)
    if fmt == "e4m3":
        vals = words.view(ml_dtypes.float8_e4m3fn).astype(np.float64)
    else:
        nib = np.empty((g, 128, n, 4), np.uint8)
        nib[..., 0::2] = words & 0xF
        nib[..., 1::2] = words >> 4
        vals = E2M1[nib]
    vals = vals * np.repeat(np.exp2(scales.astype(np.float64) - 127.0), 8, axis=1)[..., None]
    return vals.transpose(0, 1, 3, 2).reshape(g * 512, n)


def gelu(v):
    return 0.5 * v * (1.0 + np.tanh(np.sqrt(2.0 / np.pi) * (v + 0.044715 * v**3)))


K, T, S, S2 = 1024, 2048, 512, 1024


def setup_inputs():
    n = np.random.standard_normal
    s = mx_kscale(K)[:, None]
    d = {}
    d["tab_words"], d["tab_scales"] = pack_weight(n((K, T)) * s, "e4m3")
    d["offs"] = striped(np.random.permutation(T)[:S])
    d["offs2"] = striped(np.random.permutation(T)[:S2])
    d["wa"] = (n((K, K)) / K / s / s.T).astype(np.float32)
    d["wb_words"], d["wb_scales"] = pack_weight(n((K, K)) / K / s / s.T, "e2m1")
    d["wc"] = (n((K, K)) / K / s).astype(np.float32)
    d["gain"] = (1.3 * np.exp(0.3 * n(K)) / s[:, 0]).astype(np.float32)
    d["base"] = (0.5 * n(S2)).astype(np.float32)
    return d


def reference(tab_words, tab_scales, offs, offs2, wa, wb_words, wb_scales, wc, gain, base):
    TW = unpack_weight(tab_words, tab_scales, "e4m3")
    v = TW[:, unstriped(offs)]
    v2 = TW[:, unstriped(offs2)]
    wb = unpack_weight(wb_words, wb_scales, "e2m1")
    ha = mxq(f64(wa), 0, "e4m3").T @ v
    hb = wb.T @ v
    low = np.minimum(ha, hb)
    mild = (mxq(f64(wc), 0, "e4m3").T @ v) * f64(gain)[:, None]
    e1 = v2.T @ mxq(low, 0, "e4m3")
    e2 = v2.T @ mxq(mild, 0, "e4m3")
    return e1 / (1.0 + np.abs(e2)) + f64(base)[:, None]

@@ -1,0 +1,281 @@
+from contextlib import ExitStack
+
+import concourse.mybir as mybir
+
+K, T, S, S2 = 1024, 2048, 512, 1024
+FLOPS = 2 * K * K * S * 3 + 2 * K * S2 * S * 2
+
+F32 = mybir.dt.float32
+BF16 = mybir.dt.bfloat16
+I32 = mybir.dt.int32
+U32 = mybir.dt.uint32
+U16 = mybir.dt.uint16
+U8 = mybir.dt.uint8
+FP8X4 = mybir.dt.float8_e4m3fn_x4
+FP4X4 = mybir.dt.float4_e2m1fn_x4
+ALU = mybir.AluOpType
+ACT = mybir.ActivationFunctionType
+
+P = 128
+PACK = 4
+KP = P * PACK
+PASSES = K // KP
+JQ = 128
+HALF = KP // 2
+
+
+def tile_list_tank_mate_scores_kernel(tc, tab_words, tab_scales, offs, offs2, wa, wb_words, wb_scales, wc, gain, base, out):
+    nc = tc.nc
+    with ExitStack() as ctx:
+        keep = ctx.enter_context(tc.tile_pool(name="keep", bufs=1))
+        ring = ctx.enter_context(tc.tile_pool(name="ring", bufs=3))
+        psum = ctx.enter_context(tc.psum_pool(name="psum", bufs=1))
+
+        offs_t = keep.tile([P, S // 16], U16, name="offs_t")
+        offs2_t = keep.tile([P, S2 // 16], U16, name="offs2_t")
+        tab_s = keep.tile([P, T], U8, name="tab_s", align_bytes=64)
+        wb_s_raw = keep.tile([P, K], U8, name="wb_s_raw", align_bytes=64)
+        wb_w_raw = keep.tile([P, PASSES, 2 * K], U8, name="wb_w_raw", align_bytes=64)
+        tab_w = [keep.tile([P, T], U32, name=f"tab_w{a}", align_bytes=64) for a in range(PASSES)]
+        gain_t = keep.tile([P, PASSES, PACK], F32, name="gain_t")
+        base_t = keep.tile([P, S2 // P], F32, name="base_t")
+        v_s_low = keep.tile([P, S], U8, name="v_s_low", align_bytes=64)
+        wb_s_low = keep.tile([P, K], U8, name="wb_s_low", align_bytes=64)
+        banks = [psum.tile([P, S], F32, name=f"bank{i}") for i in range(8)]
+        used_banks = []
+
+        def next_bank():
+            used_banks.append(banks[len(used_banks) % len(banks)])
+            return used_banks[-1]
+
+        nc.vector.memset(tab_s[:].bitcast(I32), 0)
+        nc.vector.memset(wb_s_raw[:].bitcast(I32), 0)
+        nc.vector.memset(v_s_low[96:P, :].bitcast(I32), 0)
+        nc.vector.memset(wb_s_low[96:P, :].bitcast(I32), 0)
+
+        raw_ring = [keep.tile([P, PACK, HALF], F32, name=f"raw{i}") for i in range(16)]
+        raw = {}
+
+        def load_w(name, a, b, h):
+            w = wa if name == "wa" else wc
+            t = raw_ring[len(raw) % len(raw_ring)]
+            c0 = b * KP + h * HALF
+            nc.sync.dma_start(out=t[:], in_=w[a * KP:(a + 1) * KP, c0:c0 + HALF].rearrange("(p j) c -> p j c", j=PACK))
+            raw[(name, a, b, h)] = t
+
+        def load_tab(a):
+            nc.sync.dma_start(out=tab_w[a][:].bitcast(I32), in_=tab_words[a].rearrange("p t i -> p (t i)").bitcast(I32))
+
+        def load_scales(eng, dst, src, q):
+            eng.dma_start(out=dst[32 * q:32 * q + 8, :].bitcast(I32), in_=src[:, 4 * q:4 * q + 4, :].bitcast(I32))
+
+        def shift_rows(eng, dst, src):
+            eng.dma_start(out=dst[0:P - 4, :].bitcast(I32), in_=src[4:P, :].bitcast(I32))
+
+        pre = [keep.tile([P, PACK * KP], BF16, name=f"pre{i}", align_bytes=64) for i in range(6)]
+        slot = {("wc", 0, 0): 0, ("wc", 1, 0): 1, ("wc", 0, 1): 2, ("wc", 1, 1): 3, ("mild", 0): 4, ("mild", 1): 5,
+                ("wa", 0, 0): 0, ("wa", 1, 0): 2, ("wa", 0, 1): 3, ("wa", 1, 1): 4, ("low", 0): 1, ("low", 1): 5}
+        codes = {}
+        scales = {}
+
+        def cast(name, a, b, h, eng):
+            g = pre[slot[(name, a, b)]][:].rearrange("p (t m j) -> p t m j", t=PACK, j=PACK)
+            pieces = 1 if eng == "g" else 1
+            step = 64 // pieces
+            for i in range(pieces):
+                dst = g[:, :, h * 64 + i * step:h * 64 + (i + 1) * step, :].rearrange("p t m j -> p m t j")
+                src = raw[(name, a, b, h)][:, :, i * step * PACK:(i + 1) * step * PACK].rearrange("p j (m t) -> p m t j", t=PACK)
+                if eng == "s":
+                    nc.scalar.copy(out=dst, in_=src)
+                elif eng == "v":
+                    nc.vector.tensor_copy(out=dst, in_=src)
+                else:
+                    nc.gpsimd.tensor_scalar(dst, src, 1.0, 0.0, ALU.mult, ALU.add)
+
+        def quant(*key):
+            codes[key] = keep.tile([P, KP], U32, name="codes_" + "".join(map(str, key)), align_bytes=64)
+            scales[key] = keep.tile([P, KP], U8, name="scales_" + "".join(map(str, key)), align_bytes=64)
+            nc.vector.quantize_mx(out=codes[key][:].bitcast(FP8X4), scales=scales[key][:], in_=pre[slot[key]][:])
+
+        v_w = [keep.tile([P, S], U32, name=f"v_w{a}", align_bytes=64) for a in range(PASSES)]
+        v2_w = [[keep.tile([P, S], U32, name=f"v2_w{a}{h}", align_bytes=64) for h in range(2)] for a in range(PASSES)]
+        v_s = keep.tile([P, S], U8, name="v_s", align_bytes=64)
+        v2_s = [keep.tile([P, S], U8, name=f"v2_s{h}", align_bytes=64) for h in range(2)]
+        wb_w = keep.tile([P, PASSES, 2 * K], U8, name="wb_w", align_bytes=64)
+        wb_s = keep.tile([P, K], U8, name="wb_s", align_bytes=64)
+        offs2_half = [offs2_t[:, 32 * h:32 * (h + 1)] for h in range(2)]
+
+        def first_stage(name, b, jq):
+            bank = next_bank()[:].rearrange("p (t n) -> p t n", t=PACK)
+            js = slice(jq * JQ, (jq + 1) * JQ)
+            for t in range(PACK):
+                for a in range(PASSES):
+                    if name == "wb":
+                        c0 = b * KP + t * P
+                        lhs = wb_w[:, a, 2 * c0:2 * (c0 + P)].bitcast(FP4X4)
+                        lhs_s = (wb_s, wb_s_low)[a][:, c0:c0 + P]
+                        rhs_s = (v_s, v_s_low)[a][:, js]
+                    else:
+                        lhs = codes[(name, a, b)][:, t * P:(t + 1) * P].bitcast(FP8X4)
+                        lhs_s = scales[(name, a, b)][:, t * P:(t + 1) * P]
+                        rhs_s = v_s[4 * a:P, js]
+                    nc.tensor.matmul_mx(out=bank[:, t, :], lhsT=lhs, lhsT_scale=lhs_s, rhs=v_w[a][:, js].bitcast(FP8X4),
+                                        rhs_scale=rhs_s, start=(a == 0), stop=(a == PASSES - 1))
+            return bank.rearrange("p t n -> p n t")
+
+        hb = [keep.tile([P, S, PACK], F32, name=f"hb{b}") for b in range(PASSES)]
+
+        def pre_cols(key, jq):
+            return pre[slot[key]][:, jq * JQ * PACK:(jq + 1) * JQ * PACK].rearrange("p (n t) -> p n t", t=PACK)
+
+        def make_hb(b, jq):
+            nc.scalar.copy(out=hb[b][:, jq * JQ:(jq + 1) * JQ, :], in_=first_stage("wb", b, jq))
+
+        def make_mild(b, jq):
+            nc.vector.tensor_tensor(pre_cols(("mild", b), jq), first_stage("wc", b, jq),
+                                    gain_t[:, b:b + 1, :].to_broadcast([P, JQ, PACK]), ALU.mult)
+
+        def make_low(b, jq):
+            nc.vector.tensor_tensor(pre_cols(("low", b), jq), first_stage("wa", b, jq), hb[b][:, jq * JQ:(jq + 1) * JQ, :], ALU.min)
+
+        def second_stage(name, u):
+            bank = next_bank()
+            h, ms = u // 4, slice(u % 4 * P, (u % 4 + 1) * P)
+            for b in range(PASSES):
+                nc.tensor.matmul_mx(out=bank[:], lhsT=v2_w[b][h][:, ms].bitcast(FP8X4), lhsT_scale=v2_s[h][4 * b:P, ms],
+                                    rhs=codes[(name, b)][:].bitcast(FP8X4), rhs_scale=scales[(name, b)][:],
+                                    start=(b == 0), stop=(b == PASSES - 1))
+            return bank[:]
+
+        damp = [keep.tile([P, S], F32, name=f"damp{u}") for u in range(S2 // P)]
+        mag = {}
+
+        def make_mag(u):
+            mag[u] = ring.tile([P, S], F32, name=f"mag{u}", tag="mag")
+            nc.scalar.activation(mag[u][:], second_stage("mild", u), ACT.Abs)
+
+        def make_damp(u):
+            root = ring.tile([P, S], F32, name=f"root{u}", tag="root")
+            nc.scalar.activation(root[:], mag[u][:], ACT.Abs_reciprocal_sqrt, bias=1.0)
+            nc.scalar.activation(damp[u][:], root[:], ACT.Square)
+
+        def finish(u):
+            prod = ring.tile([P, S], F32, name=f"prod{u}", tag="prod")
+            nc.vector.tensor_tensor(prod[:], second_stage("low", u), damp[u][:], ALU.mult)
+            res = keep.tile([P, S], F32, name=f"res{u}")
+            nc.gpsimd.tensor_scalar(res[:], prod[:], 1.0, base_t[:, u:u + 1], ALU.mult, ALU.add)
+            nc.sync.dma_start(out=out[u * P:(u + 1) * P, :], in_=res[:])
+
+        def gather(dst, src, lst):
+            nc.vector.tensor_copy(dst[:], src[:].indirect(lst))
+
+        def deal_wb_words():
+            nc.vector.tensor_copy(out=wb_w[:].rearrange("p a c -> p (a c)").bitcast(U16).rearrange("p (b t m) -> p b t m", t=PACK, m=P),
+                                  in_=wb_w_raw[:].rearrange("p a c -> p (a c)").bitcast(U16).rearrange("p (b m t) -> p b t m", t=PACK, m=P))
+
+        def deal_wb_scales():
+            nc.vector.tensor_copy(out=wb_s[:].rearrange("p (b t m) -> p b t m", b=2, t=PACK),
+                                  in_=wb_s_raw[:].rearrange("p (b m t) -> p b t m", b=2, t=PACK))
+
+        nc.sync.dma_start(offs_t[:], offs)
+        nc.sync.dma_start(offs2_t[:], offs2)
+        tab_s_in = keep.tile([P, T], U8, name="tab_s_in", align_bytes=64)
+        for q in range(4): load_scales(nc.sync, tab_s_in, tab_scales, q)
+        nc.sync.dma_start(out=wb_w_raw[:].bitcast(I32), in_=wb_words.rearrange("a p c -> p a c").bitcast(I32))
+        load_tab(0)
+        for q in range(4): load_scales(nc.sync, wb_s_raw, wb_scales, q)
+        load_tab(1)
+        for h in range(2): load_w("wc", 0, 0, h)
+        for q in range(4): nc.vector.tensor_copy(tab_s[32 * q:32 * q + 8, :].bitcast(I32), tab_s_in[32 * q:32 * q + 8, :].bitcast(I32))
+        gather(v_s, tab_s, offs_t[:])
+        deal_wb_words()
+        deal_wb_scales()
+        shift_rows(nc.scalar, v_s_low, v_s)
+        shift_rows(nc.scalar, wb_s_low, wb_s)
+        nc.sync.dma_start(out=gain_t[:], in_=gain.rearrange("(b p t) -> p b t", p=P, t=PACK))
+        for h in range(2): load_w("wc", 1, 0, h)
+        for h in range(2): load_w("wc", 0, 1, h)
+        for h in range(2): load_w("wc", 1, 1, h)
+        for h in range(2): load_w("wa", 0, 0, h)
+        for h in range(2): load_w("wa", 1, 0, h)
+        for h in range(2): load_w("wa", 0, 1, h)
+        for h in range(2): load_w("wa", 1, 1, h)
+        with nc.allow_non_contiguous_dma(reason="one base value for each partition and output tile"):
+            nc.sync.dma_start(out=base_t[:], in_=base.rearrange("(u p) -> p u", p=P))
+        gather(v_w[0], tab_w[0], offs_t[:])
+        gather(v2_s[0], tab_s, offs2_half[0])
+        gather(v_w[1], tab_w[1], offs_t[:])
+        cast("wc", 0, 0, 0, "s")
+        cast("wc", 0, 0, 1, "s")
+        gather(v2_w[0][0], tab_w[0], offs2_half[0])
+        gather(v2_w[1][0], tab_w[1], offs2_half[0])
+        cast("wc", 1, 0, 0, "s")
+        quant("wc", 0, 0)
+        gather(v2_s[1], tab_s, offs2_half[1])
+        cast("wc", 1, 0, 1, "v")
+        make_hb(0, 0)
+        cast("wc", 0, 1, 0, "s")
+        quant("wc", 1, 0)
+        cast("wc", 0, 1, 1, "s")
+        gather(v2_w[0][1], tab_w[0], offs2_half[1])
+        make_hb(0, 1)
+        cast("wc", 1, 1, 0, "s")
+        quant("wc", 0, 1)
+        cast("wc", 1, 1, 1, "v")
+        make_mild(0, 0)
+        make_mild(0, 1)
+        quant("wc", 1, 1)
+        make_hb(0, 2)
+        make_mild(0, 2)
+        make_hb(0, 3)
+        make_mild(0, 3)
+        cast("wa", 0, 0, 0, "s")
+        make_mild(1, 0)
+        quant("mild", 0)
+        make_hb(1, 0)
+        make_mild(1, 1)
+        cast("wa", 0, 0, 1, "s")
+        make_mild(1, 2)
+        make_hb(1, 1)
+        make_mild(1, 3)
+        cast("wa", 1, 0, 0, "s")
+        cast("wa", 1, 0, 1, "v")
+        make_hb(1, 2)
+        quant("mild", 1)
+        make_hb(1, 3)
+        quant("wa", 0, 0)
+        cast("wa", 0, 1, 0, "s")
+        gather(v2_w[1][1], tab_w[1], offs2_half[1])
+        quant("wa", 1, 0)
+        make_mag(0)
+        make_mag(1)
+        cast("wa", 0, 1, 1, "v")
+        cast("wa", 1, 1, 0, "s")
+        cast("wa", 1, 1, 1, "v")
+        make_damp(0)
+        make_low(0, 0)
+        quant("wa", 0, 1)
+        make_low(0, 1)
+        make_mag(2)
+        make_damp(1)
+        quant("wa", 1, 1)
+        make_low(0, 2)
+        make_low(0, 3)
+        make_mag(3)
+        make_damp(2)
+        make_low(1, 0)
+        quant("low", 0)
+        make_low(1, 1)
+        make_mag(4)
+        make_damp(3)
+        make_low(1, 2)
+        make_low(1, 3)
+        make_mag(5)
+        make_damp(4)
+        quant("low", 1)
+        make_mag(6)
+        make_damp(5)
+        make_mag(7)
+        make_damp(6)
+        make_damp(7)
+        for u in range(8): finish(u)

@@ -36,35 +36,39 @@ def tile_list_tank_mate_scores_kernel(tc, tab_words, tab_scales, offs, offs2, wa
         tab_s = keep.tile([P, T], U8, name="tab_s", align_bytes=64)
         wb_s_raw = keep.tile([P, K], U8, name="wb_s_raw", align_bytes=64)
         wb_w_raw = keep.tile([P, PASSES, 2 * K], U8, name="wb_w_raw", align_bytes=64)
-        tab_w = [keep.tile([P, T], U32, name=f"tab_w{a}", align_bytes=64) for a in range(PASSES)]
+        tab_w = keep.tile([P, PASSES, T], U32, name="tab_w", align_bytes=64)
         gain_t = keep.tile([P, PASSES, PACK], F32, name="gain_t")
         base_t = keep.tile([P, S2 // P], F32, name="base_t")
         v_s_low = keep.tile([P, S], U8, name="v_s_low", align_bytes=64)
         wb_s_low = keep.tile([P, K], U8, name="wb_s_low", align_bytes=64)
         banks = [psum.tile([P, S], F32, name=f"bank{i}") for i in range(8)]
-        used_banks = []
+        used_banks = {"scalar": [], "vector": []}
 
-        def next_bank():
-            used_banks.append(banks[len(used_banks) % len(banks)])
-            return used_banks[-1]
+        def next_bank(reader):
+            first = 0 if reader == "scalar" else 4
+            used_banks[reader].append(banks[first + len(used_banks[reader]) % 4])
+            return used_banks[reader][-1]
 
         nc.vector.memset(tab_s[:].bitcast(I32), 0)
         nc.vector.memset(wb_s_raw[:].bitcast(I32), 0)
         nc.vector.memset(v_s_low[96:P, :].bitcast(I32), 0)
         nc.vector.memset(wb_s_low[96:P, :].bitcast(I32), 0)
 
-        raw_ring = [keep.tile([P, PACK, HALF], F32, name=f"raw{i}") for i in range(16)]
+        raw_tiles = [keep.tile([P, PACK, KP], F32, name=f"raw{i}") for i in range(8)]
+        raw_slot = {("wc", 0, 0): 0, ("wc", 1, 0): 1, ("wc", 0, 1): 2, ("wc", 1, 1): 3,
+                    ("wa", 0, 0): 4, ("wa", 1, 0): 5, ("wa", 0, 1): 6, ("wa", 1, 1): 7}
         raw = {}
 
-        def load_w(name, a, b, h):
+        def load_w(name, a, b, h0=0, h1=2):
             w = wa if name == "wa" else wc
-            t = raw_ring[len(raw) % len(raw_ring)]
-            c0 = b * KP + h * HALF
-            nc.sync.dma_start(out=t[:], in_=w[a * KP:(a + 1) * KP, c0:c0 + HALF].rearrange("(p j) c -> p j c", j=PACK))
-            raw[(name, a, b, h)] = t
+            t = raw_tiles[raw_slot[(name, a, b)]]
+            cols = slice(b * KP + h0 * HALF, b * KP + h1 * HALF)
+            nc.sync.dma_start(out=t[:, :, h0 * HALF:h1 * HALF], in_=w[a * KP:(a + 1) * KP, cols].rearrange("(p j) c -> p j c", j=PACK))
+            for h in range(h0, h1):
+                raw[(name, a, b, h)] = t[:, :, h * HALF:(h + 1) * HALF]
 
-        def load_tab(a):
-            nc.sync.dma_start(out=tab_w[a][:].bitcast(I32), in_=tab_words[a].rearrange("p t i -> p (t i)").bitcast(I32))
+        def load_tab():
+            nc.sync.dma_start(out=tab_w[:].bitcast(I32), in_=tab_words.rearrange("a p t i -> p a (t i)").bitcast(I32))
 
         def load_scales(eng, dst, src, q):
             eng.dma_start(out=dst[32 * q:32 * q + 8, :].bitcast(I32), in_=src[:, 4 * q:4 * q + 4, :].bitcast(I32))
@@ -78,13 +82,12 @@ def tile_list_tank_mate_scores_kernel(tc, tab_words, tab_scales, offs, offs2, wa
         codes = {}
         scales = {}
 
-        def cast(name, a, b, h, eng):
+        def cast(name, a, b, h, eng, part=(0, 4)):
             g = pre[slot[(name, a, b)]][:].rearrange("p (t m j) -> p t m j", t=PACK, j=PACK)
-            pieces = 1 if eng == "g" else 1
-            step = 64 // pieces
-            for i in range(pieces):
-                dst = g[:, :, h * 64 + i * step:h * 64 + (i + 1) * step, :].rearrange("p t m j -> p m t j")
-                src = raw[(name, a, b, h)][:, :, i * step * PACK:(i + 1) * step * PACK].rearrange("p j (m t) -> p m t j", t=PACK)
+            spans = [(i, i + 1) for i in range(part[0], part[1], 1)] if eng == "g" else [part]
+            for i0, i1 in spans:
+                dst = g[:, :, h * 64 + i0 * 16:h * 64 + i1 * 16, :].rearrange("p t m j -> p m t j")
+                src = raw[(name, a, b, h)][:, :, i0 * 64:i1 * 64].rearrange("p j (m t) -> p m t j", t=PACK)
                 if eng == "s":
                     nc.scalar.copy(out=dst, in_=src)
                 elif eng == "v":
@@ -98,15 +101,14 @@ def tile_list_tank_mate_scores_kernel(tc, tab_words, tab_scales, offs, offs2, wa
             nc.vector.quantize_mx(out=codes[key][:].bitcast(FP8X4), scales=scales[key][:], in_=pre[slot[key]][:])
 
         v_w = [keep.tile([P, S], U32, name=f"v_w{a}", align_bytes=64) for a in range(PASSES)]
-        v2_w = [[keep.tile([P, S], U32, name=f"v2_w{a}{h}", align_bytes=64) for h in range(2)] for a in range(PASSES)]
+        v2_w = [keep.tile([P, S2], U32, name=f"v2_w{a}", align_bytes=64) for a in range(PASSES)]
         v_s = keep.tile([P, S], U8, name="v_s", align_bytes=64)
-        v2_s = [keep.tile([P, S], U8, name=f"v2_s{h}", align_bytes=64) for h in range(2)]
+        v2_s = keep.tile([P, S2], U8, name="v2_s", align_bytes=64)
         wb_w = keep.tile([P, PASSES, 2 * K], U8, name="wb_w", align_bytes=64)
         wb_s = keep.tile([P, K], U8, name="wb_s", align_bytes=64)
-        offs2_half = [offs2_t[:, 32 * h:32 * (h + 1)] for h in range(2)]
 
         def first_stage(name, b, jq):
-            bank = next_bank()[:].rearrange("p (t n) -> p t n", t=PACK)
+            bank = next_bank("scalar" if name == "wb" else "vector")[:].rearrange("p (t n) -> p t n", t=PACK)
             js = slice(jq * JQ, (jq + 1) * JQ)
             for t in range(PACK):
                 for a in range(PASSES):
@@ -123,7 +125,7 @@ def tile_list_tank_mate_scores_kernel(tc, tab_words, tab_scales, offs, offs2, wa
                                         rhs_scale=rhs_s, start=(a == 0), stop=(a == PASSES - 1))
             return bank.rearrange("p t n -> p n t")
 
-        hb = [keep.tile([P, S, PACK], F32, name=f"hb{b}") for b in range(PASSES)]
+        hb = [raw_tiles[3 * b][:].rearrange("p j c -> p (j c)").rearrange("p (n t) -> p n t", t=PACK) for b in range(PASSES)]
 
         def pre_cols(key, jq):
             return pre[slot[key]][:, jq * JQ * PACK:(jq + 1) * JQ * PACK].rearrange("p (n t) -> p n t", t=PACK)
@@ -139,10 +141,10 @@ def tile_list_tank_mate_scores_kernel(tc, tab_words, tab_scales, offs, offs2, wa
             nc.vector.tensor_tensor(pre_cols(("low", b), jq), first_stage("wa", b, jq), hb[b][:, jq * JQ:(jq + 1) * JQ, :], ALU.min)
 
         def second_stage(name, u):
-            bank = next_bank()
-            h, ms = u // 4, slice(u % 4 * P, (u % 4 + 1) * P)
+            bank = next_bank("scalar" if name == "mild" else "vector")
+            ms = slice(u * P, (u + 1) * P)
             for b in range(PASSES):
-                nc.tensor.matmul_mx(out=bank[:], lhsT=v2_w[b][h][:, ms].bitcast(FP8X4), lhsT_scale=v2_s[h][4 * b:P, ms],
+                nc.tensor.matmul_mx(out=bank[:], lhsT=v2_w[b][:, ms].bitcast(FP8X4), lhsT_scale=v2_s[4 * b:P, ms],
                                     rhs=codes[(name, b)][:].bitcast(FP8X4), rhs_scale=scales[(name, b)][:],
                                     start=(b == 0), stop=(b == PASSES - 1))
             return bank[:]
@@ -157,17 +159,24 @@ def tile_list_tank_mate_scores_kernel(tc, tab_words, tab_scales, offs, offs2, wa
         def make_damp(u):
             root = ring.tile([P, S], F32, name=f"root{u}", tag="root")
             nc.scalar.activation(root[:], mag[u][:], ACT.Abs_reciprocal_sqrt, bias=1.0)
-            nc.scalar.activation(damp[u][:], root[:], ACT.Square)
+            if u in (2, 3, 4, 5):
+                for c in range(0, S, S // 2):
+                    nc.gpsimd.tensor_tensor(damp[u][:, c:c + S // 2], root[:, c:c + S // 2], root[:, c:c + S // 2], ALU.mult)
+            else:
+                nc.scalar.activation(damp[u][:], root[:], ACT.Square)
 
         def finish(u):
             prod = ring.tile([P, S], F32, name=f"prod{u}", tag="prod")
             nc.vector.tensor_tensor(prod[:], second_stage("low", u), damp[u][:], ALU.mult)
             res = keep.tile([P, S], F32, name=f"res{u}")
-            nc.gpsimd.tensor_scalar(res[:], prod[:], 1.0, base_t[:, u:u + 1], ALU.mult, ALU.add)
+            if u < 6:
+                nc.gpsimd.tensor_scalar(res[:], prod[:], 1.0, base_t[:, u:u + 1], ALU.mult, ALU.add)
+            else:
+                nc.scalar.activation(res[:], prod[:], ACT.Identity, bias=base_t[:, u:u + 1])
             nc.sync.dma_start(out=out[u * P:(u + 1) * P, :], in_=res[:])
 
         def gather(dst, src, lst):
-            nc.vector.tensor_copy(dst[:], src[:].indirect(lst))
+            nc.vector.tensor_copy(dst[:], src.indirect(lst[:]))
 
         def deal_wb_words():
             nc.vector.tensor_copy(out=wb_w[:].rearrange("p a c -> p (a c)").bitcast(U16).rearrange("p (b t m) -> p b t m", t=PACK, m=P),
@@ -177,89 +186,83 @@ def tile_list_tank_mate_scores_kernel(tc, tab_words, tab_scales, offs, offs2, wa
             nc.vector.tensor_copy(out=wb_s[:].rearrange("p (b t m) -> p b t m", b=2, t=PACK),
                                   in_=wb_s_raw[:].rearrange("p (b m t) -> p b t m", b=2, t=PACK))
 
+        warm = keep.tile([P, 2], F32, name="warm")
+        nc.vector.memset(warm[:, 0:1], 1.0)
+        nc.scalar.activation(warm[:, 1:2], warm[:, 0:1], ACT.Abs_reciprocal_sqrt, bias=1.0)
         nc.sync.dma_start(offs_t[:], offs)
         nc.sync.dma_start(offs2_t[:], offs2)
         tab_s_in = keep.tile([P, T], U8, name="tab_s_in", align_bytes=64)
         for q in range(4): load_scales(nc.sync, tab_s_in, tab_scales, q)
         nc.sync.dma_start(out=wb_w_raw[:].bitcast(I32), in_=wb_words.rearrange("a p c -> p a c").bitcast(I32))
-        load_tab(0)
-        for q in range(4): load_scales(nc.sync, wb_s_raw, wb_scales, q)
-        load_tab(1)
-        for h in range(2): load_w("wc", 0, 0, h)
-        for q in range(4): nc.vector.tensor_copy(tab_s[32 * q:32 * q + 8, :].bitcast(I32), tab_s_in[32 * q:32 * q + 8, :].bitcast(I32))
-        gather(v_s, tab_s, offs_t[:])
-        deal_wb_words()
-        deal_wb_scales()
-        shift_rows(nc.scalar, v_s_low, v_s)
-        shift_rows(nc.scalar, wb_s_low, wb_s)
+        load_tab()
+        for q in range(4): load_scales(nc.scalar, wb_s_raw, wb_scales, q)
+        load_w("wc", 0, 0)
         nc.sync.dma_start(out=gain_t[:], in_=gain.rearrange("(b p t) -> p b t", p=P, t=PACK))
-        for h in range(2): load_w("wc", 1, 0, h)
-        for h in range(2): load_w("wc", 0, 1, h)
-        for h in range(2): load_w("wc", 1, 1, h)
-        for h in range(2): load_w("wa", 0, 0, h)
-        for h in range(2): load_w("wa", 1, 0, h)
-        for h in range(2): load_w("wa", 0, 1, h)
-        for h in range(2): load_w("wa", 1, 1, h)
+        load_w("wc", 1, 0)
+        load_w("wc", 0, 1)
+        load_w("wc", 1, 1)
+        load_w("wa", 0, 0)
+        load_w("wa", 1, 0)
+        load_w("wa", 0, 1)
+        load_w("wa", 1, 1, 0, 1)
+        load_w("wa", 1, 1, 1, 2)
         with nc.allow_non_contiguous_dma(reason="one base value for each partition and output tile"):
             nc.sync.dma_start(out=base_t[:], in_=base.rearrange("(u p) -> p u", p=P))
-        gather(v_w[0], tab_w[0], offs_t[:])
-        gather(v2_s[0], tab_s, offs2_half[0])
-        gather(v_w[1], tab_w[1], offs_t[:])
+        for q in range(4): nc.vector.tensor_copy(tab_s[32 * q:32 * q + 8, :].bitcast(I32), tab_s_in[32 * q:32 * q + 8, :].bitcast(I32))
+        gather(v_s, tab_s[:], offs_t)
+        shift_rows(nc.scalar, v_s_low, v_s)
+        deal_wb_words()
+        deal_wb_scales()
+        shift_rows(nc.scalar, wb_s_low, wb_s)
+        gather(v_w[0], tab_w[:, 0, :], offs_t)
+        gather(v_w[1], tab_w[:, 1, :], offs_t)
+        gather(v2_s, tab_s[:], offs2_t)
+        gather(v2_w[0], tab_w[:, 0, :], offs2_t)
+        gather(v2_w[1], tab_w[:, 1, :], offs2_t)
         cast("wc", 0, 0, 0, "s")
-        cast("wc", 0, 0, 1, "s")
-        gather(v2_w[0][0], tab_w[0], offs2_half[0])
-        gather(v2_w[1][0], tab_w[1], offs2_half[0])
+        cast("wc", 0, 0, 1, "g")
         cast("wc", 1, 0, 0, "s")
+        cast("wc", 1, 0, 1, "g")
         quant("wc", 0, 0)
-        gather(v2_s[1], tab_s, offs2_half[1])
-        cast("wc", 1, 0, 1, "v")
-        make_hb(0, 0)
-        cast("wc", 0, 1, 0, "s")
         quant("wc", 1, 0)
-        cast("wc", 0, 1, 1, "s")
-        gather(v2_w[0][1], tab_w[0], offs2_half[1])
-        make_hb(0, 1)
+        for jq in range(4): make_hb(0, jq)
+        cast("wc", 0, 1, 0, "s")
+        cast("wc", 0, 1, 1, "g")
         cast("wc", 1, 1, 0, "s")
-        quant("wc", 0, 1)
-        cast("wc", 1, 1, 1, "v")
+        cast("wc", 1, 1, 1, "g")
         make_mild(0, 0)
         make_mild(0, 1)
-        quant("wc", 1, 1)
-        make_hb(0, 2)
+        quant("wc", 0, 1)
         make_mild(0, 2)
-        make_hb(0, 3)
+        quant("wc", 1, 1)
         make_mild(0, 3)
-        cast("wa", 0, 0, 0, "s")
+        for jq in range(4): make_hb(1, jq)
         make_mild(1, 0)
         quant("mild", 0)
-        make_hb(1, 0)
         make_mild(1, 1)
-        cast("wa", 0, 0, 1, "s")
         make_mild(1, 2)
-        make_hb(1, 1)
         make_mild(1, 3)
+        cast("wa", 0, 0, 0, "s")
+        cast("wa", 0, 0, 1, "g")
         cast("wa", 1, 0, 0, "s")
-        cast("wa", 1, 0, 1, "v")
-        make_hb(1, 2)
-        quant("mild", 1)
-        make_hb(1, 3)
+        cast("wa", 1, 0, 1, "g")
         quant("wa", 0, 0)
-        cast("wa", 0, 1, 0, "s")
-        gather(v2_w[1][1], tab_w[1], offs2_half[1])
-        quant("wa", 1, 0)
+        quant("mild", 1)
         make_mag(0)
         make_mag(1)
+        cast("wa", 0, 1, 0, "g")
         cast("wa", 0, 1, 1, "v")
-        cast("wa", 1, 1, 0, "s")
-        cast("wa", 1, 1, 1, "v")
+        quant("wa", 1, 0)
         make_damp(0)
+        cast("wa", 1, 1, 0, "g")
         make_low(0, 0)
-        quant("wa", 0, 1)
+        cast("wa", 1, 1, 1, "v")
         make_low(0, 1)
+        quant("wa", 0, 1)
         make_mag(2)
         make_damp(1)
-        quant("wa", 1, 1)
         make_low(0, 2)
+        quant("wa", 1, 1)
         make_low(0, 3)
         make_mag(3)
         make_damp(2)

@@ -20,92 +20,134 @@ P = 128
 PACK = 4
 KP = P * PACK
 PASSES = K // KP
-JQ = 128
-HALF = KP // 2
+QUADRANTS = 4
+JQ = S // PACK
+QUARTERS = S // JQ
+TILES = S2 // P
+assert TILES == PASSES * QUARTERS
+READER_BANKS = 4
+SHIFT_ROWS = 112
+ROUNDED_TILES = 5
+STEP_BUFS = 3
+GPSIMD_SQUARES = range(3, 6)
+SCALAR_BASE_TILES = 2
 
 
 def tile_list_tank_mate_scores_kernel(tc, tab_words, tab_scales, offs, offs2, wa, wb_words, wb_scales, wc, gain, base, out):
     nc = tc.nc
+    chunks = [(a, b) for b in range(PASSES) for a in range(PASSES)]
     with ExitStack() as ctx:
         keep = ctx.enter_context(tc.tile_pool(name="keep", bufs=1))
-        ring = ctx.enter_context(tc.tile_pool(name="ring", bufs=3))
+        steps = ctx.enter_context(tc.tile_pool(name="steps", bufs=STEP_BUFS))
         psum = ctx.enter_context(tc.psum_pool(name="psum", bufs=1))
+
+        def held(shape, dtype, name, tag=None):
+            return keep.tile(shape, dtype, name=name, tag=tag or name, align_bytes=64)
+
+        banks = [psum.tile([P, S], F32, name=f"bank{i}") for i in range(2 * READER_BANKS)]
+        taken = {"scalar": [], "vector": []}
+
+        def next_bank(reader):
+            first = 0 if reader == "scalar" else READER_BANKS
+            taken[reader].append(banks[first + len(taken[reader]) % READER_BANKS])
+            return taken[reader][-1]
 
         offs_t = keep.tile([P, S // 16], U16, name="offs_t")
         offs2_t = keep.tile([P, S2 // 16], U16, name="offs2_t")
-        tab_s = keep.tile([P, T], U8, name="tab_s", align_bytes=64)
-        wb_s_raw = keep.tile([P, K], U8, name="wb_s_raw", align_bytes=64)
-        wb_w_raw = keep.tile([P, PASSES, 2 * K], U8, name="wb_w_raw", align_bytes=64)
-        tab_w = keep.tile([P, PASSES, T], U32, name="tab_w", align_bytes=64)
         gain_t = keep.tile([P, PASSES, PACK], F32, name="gain_t")
-        base_t = keep.tile([P, S2 // P], F32, name="base_t")
-        v_s_low = keep.tile([P, S], U8, name="v_s_low", align_bytes=64)
-        wb_s_low = keep.tile([P, K], U8, name="wb_s_low", align_bytes=64)
-        banks = [psum.tile([P, S], F32, name=f"bank{i}") for i in range(8)]
-        used_banks = {"scalar": [], "vector": []}
+        tab_s_in = held([P, T], U8, "tab_s_in")
+        tab_s = held([P, T], U8, "tab_s")
+        tab_w = held([P, PASSES, T], U32, "tab_w")
+        wb_s_in = held([P, K], U8, "wb_s_in")
+        wb_w_in = held([P, PASSES, 2 * K], U8, "wb_w_in")
+        wb_s = held([P, K], U8, "wb_s")
+        wb_w = held([P, PASSES, 2 * K], U8, "wb_w")
+        v_s = held([P, S], U8, "v_s")
+        v2_s = held([P, S2], U8, "v2_s")
+        v_w = [held([P, S], U32, f"v_w{a}") for a in range(PASSES)]
+        v2_w = [held([P, S2], U32, f"v2_w{a}") for a in range(PASSES)]
+        v_s_pass1 = held([P, S], U8, "v_s_pass1")
+        wb_s_pass1 = held([P, K], U8, "wb_s_pass1")
 
-        def next_bank(reader):
-            first = 0 if reader == "scalar" else 4
-            used_banks[reader].append(banks[first + len(used_banks[reader]) % 4])
-            return used_banks[reader][-1]
+        def load_scales(dst, src):
+            for q in range(QUADRANTS):
+                nc.sync.dma_start(out=dst[32 * q:32 * q + 8, :].bitcast(I32), in_=src[:, 4 * q:4 * q + 4, :].bitcast(I32))
 
-        nc.vector.memset(tab_s[:].bitcast(I32), 0)
-        nc.vector.memset(wb_s_raw[:].bitcast(I32), 0)
-        nc.vector.memset(v_s_low[96:P, :].bitcast(I32), 0)
-        nc.vector.memset(wb_s_low[96:P, :].bitcast(I32), 0)
+        def shift_down(dst, src):
+            nc.sync.dma_start(out=dst[0:SHIFT_ROWS, :].bitcast(I32), in_=src[4:4 + SHIFT_ROWS, :].bitcast(I32))
 
-        raw_tiles = [keep.tile([P, PACK, KP], F32, name=f"raw{i}") for i in range(8)]
-        raw_slot = {("wc", 0, 0): 0, ("wc", 1, 0): 1, ("wc", 0, 1): 2, ("wc", 1, 1): 3,
-                    ("wa", 0, 0): 4, ("wa", 1, 0): 5, ("wa", 0, 1): 6, ("wa", 1, 1): 7}
+        def gather(dst, window, offsets):
+            nc.vector.tensor_copy(dst[:], window.indirect(offsets[:]))
+
         raw = {}
 
-        def load_w(name, a, b, h0=0, h1=2):
+        def load_weight(name, chunk, home):
+            a, b = chunk
+            raw[name, chunk] = home
             w = wa if name == "wa" else wc
-            t = raw_tiles[raw_slot[(name, a, b)]]
-            cols = slice(b * KP + h0 * HALF, b * KP + h1 * HALF)
-            nc.sync.dma_start(out=t[:, :, h0 * HALF:h1 * HALF], in_=w[a * KP:(a + 1) * KP, cols].rearrange("(p j) c -> p j c", j=PACK))
-            for h in range(h0, h1):
-                raw[(name, a, b, h)] = t[:, :, h * HALF:(h + 1) * HALF]
+            nc.sync.dma_start(out=home, in_=w[a * KP:(a + 1) * KP, b * KP:(b + 1) * KP].rearrange("(p i) c -> p i c", i=PACK))
 
-        def load_tab():
-            nc.sync.dma_start(out=tab_w[:].bitcast(I32), in_=tab_words.rearrange("a p t i -> p a (t i)").bitcast(I32))
+        nc.vector.memset(wb_s_in[:].bitcast(I32), 0)
+        nc.vector.memset(tab_s[:].bitcast(I32), 0)
+        nc.vector.memset(v_s_pass1[96:P, :].bitcast(I32), 0)
+        nc.vector.memset(wb_s_pass1[96:P, :].bitcast(I32), 0)
 
-        def load_scales(eng, dst, src, q):
-            eng.dma_start(out=dst[32 * q:32 * q + 8, :].bitcast(I32), in_=src[:, 4 * q:4 * q + 4, :].bitcast(I32))
+        warm = keep.tile([P, 2], F32, name="warm")
+        nc.vector.memset(warm[:, 0:1], 1.0)
+        nc.scalar.activation(warm[:, 1:2], warm[:, 0:1], ACT.Abs_reciprocal_sqrt, bias=1.0)
 
-        def shift_rows(eng, dst, src):
-            eng.dma_start(out=dst[0:P - 4, :].bitcast(I32), in_=src[4:P, :].bitcast(I32))
+        nc.sync.dma_start(offs_t[:], offs)
+        nc.sync.dma_start(offs2_t[:], offs2)
+        load_scales(tab_s_in, tab_scales)
+        nc.sync.dma_start(out=wb_w_in[:].bitcast(I32), in_=wb_words.rearrange("a p c -> p a c").bitcast(I32))
+        nc.sync.dma_start(out=gain_t[:], in_=gain.rearrange("(b p t) -> p b t", p=P, t=PACK))
+        load_scales(wb_s_in, wb_scales)
+        nc.sync.dma_start(out=tab_w[:].bitcast(I32), in_=tab_words.rearrange("a p t i -> p a (t i)").bitcast(I32))
+        load_weight("wc", chunks[0], held([P, PACK, KP], F32, "raw_first")[:])
 
-        pre = [keep.tile([P, PACK * KP], BF16, name=f"pre{i}", align_bytes=64) for i in range(6)]
-        slot = {("wc", 0, 0): 0, ("wc", 1, 0): 1, ("wc", 0, 1): 2, ("wc", 1, 1): 3, ("mild", 0): 4, ("mild", 1): 5,
-                ("wa", 0, 0): 0, ("wa", 1, 0): 2, ("wa", 0, 1): 3, ("wa", 1, 1): 4, ("low", 0): 1, ("low", 1): 5}
-        codes = {}
-        scales = {}
+        for q in range(QUADRANTS):
+            rows = slice(32 * q, 32 * q + 8)
+            nc.vector.tensor_copy(tab_s[rows, :].bitcast(I32), tab_s_in[rows, :].bitcast(I32))
+        gather(v_s, tab_s[:], offs_t)
+        shift_down(v_s_pass1, v_s)
+        nc.vector.tensor_copy(out=wb_s[:].rearrange("p (b t m) -> p b t m", t=PACK, m=P),
+                              in_=wb_s_in[:].rearrange("p (b m t) -> p b t m", t=PACK, m=P))
+        shift_down(wb_s_pass1, wb_s)
+        nc.vector.tensor_copy(out=wb_w[:].rearrange("p a c -> p (a c)").bitcast(U16).rearrange("p (g t m) -> p g t m", t=PACK, m=P),
+                              in_=wb_w_in[:].rearrange("p a c -> p (a c)").bitcast(U16).rearrange("p (g m t) -> p g t m", t=PACK, m=P))
+        for a in range(PASSES):
+            gather(v_w[a], tab_w[:, a, :], offs_t)
+        gather(v2_s, tab_s[:], offs2_t)
+        for a in range(PASSES):
+            gather(v2_w[a], tab_w[:, a, :], offs2_t)
 
-        def cast(name, a, b, h, eng, part=(0, 4)):
-            g = pre[slot[(name, a, b)]][:].rearrange("p (t m j) -> p t m j", t=PACK, j=PACK)
-            spans = [(i, i + 1) for i in range(part[0], part[1], 1)] if eng == "g" else [part]
-            for i0, i1 in spans:
-                dst = g[:, :, h * 64 + i0 * 16:h * 64 + i1 * 16, :].rearrange("p t m j -> p m t j")
-                src = raw[(name, a, b, h)][:, :, i0 * 64:i1 * 64].rearrange("p j (m t) -> p m t j", t=PACK)
-                if eng == "s":
-                    nc.scalar.copy(out=dst, in_=src)
-                elif eng == "v":
-                    nc.vector.tensor_copy(out=dst, in_=src)
+        load_weight("wc", chunks[1], held([P, PACK, KP], F32, "raw_second", tag="wb_s_in")[:])
+        for name, b, tag in (("wc", 1, "wb_w_in"), ("wa", 0, "tab_s")):
+            both = held([P, PASSES, PACK, KP], F32, f"raw_{name}{b}", tag=tag)
+            for a in range(PASSES):
+                load_weight(name, (a, b), both[:, a, :, :])
+
+        rounded, codes, scales = {}, {}, {}
+
+        def rounded_tile(name, key):
+            n = len(rounded)
+            rounded[name, key] = held([P, PACK * KP], BF16, f"rounded_{name}{n}", tag=f"rounded{n % ROUNDED_TILES}")
+
+        def round_weight(name, chunk, shared):
+            rounded_tile(name, chunk)
+            dst = rounded[name, chunk][:].rearrange("p (t m i) -> p m i t", t=PACK, i=PACK)
+            src = raw[name, chunk].rearrange("p i (m t) -> p m i t", t=PACK)
+            for half in range(2):
+                ts = slice(2 * half, 2 * half + 2)
+                if half == 0 or not shared:
+                    nc.scalar.copy(out=dst[:, :, :, ts], in_=src[:, :, :, ts])
                 else:
-                    nc.gpsimd.tensor_scalar(dst, src, 1.0, 0.0, ALU.mult, ALU.add)
+                    nc.vector.tensor_copy(out=dst[:, :, :, ts], in_=src[:, :, :, ts])
 
-        def quant(*key):
-            codes[key] = keep.tile([P, KP], U32, name="codes_" + "".join(map(str, key)), align_bytes=64)
-            scales[key] = keep.tile([P, KP], U8, name="scales_" + "".join(map(str, key)), align_bytes=64)
-            nc.vector.quantize_mx(out=codes[key][:].bitcast(FP8X4), scales=scales[key][:], in_=pre[slot[key]][:])
-
-        v_w = [keep.tile([P, S], U32, name=f"v_w{a}", align_bytes=64) for a in range(PASSES)]
-        v2_w = [keep.tile([P, S2], U32, name=f"v2_w{a}", align_bytes=64) for a in range(PASSES)]
-        v_s = keep.tile([P, S], U8, name="v_s", align_bytes=64)
-        v2_s = keep.tile([P, S2], U8, name="v2_s", align_bytes=64)
-        wb_w = keep.tile([P, PASSES, 2 * K], U8, name="wb_w", align_bytes=64)
-        wb_s = keep.tile([P, K], U8, name="wb_s", align_bytes=64)
+        def quantize(name, key):
+            codes[name, key] = held([P, KP], U32, f"codes_{name}{len(codes)}")
+            scales[name, key] = held([P, KP], U8, f"scales_{name}{len(scales)}")
+            nc.vector.quantize_mx(out=codes[name, key][:].bitcast(FP8X4), scales=scales[name, key][:], in_=rounded[name, key][:])
 
         def first_stage(name, b, jq):
             bank = next_bank("scalar" if name == "wb" else "vector")[:].rearrange("p (t n) -> p t n", t=PACK)
@@ -115,170 +157,102 @@ def tile_list_tank_mate_scores_kernel(tc, tab_words, tab_scales, offs, offs2, wa
                     if name == "wb":
                         c0 = b * KP + t * P
                         lhs = wb_w[:, a, 2 * c0:2 * (c0 + P)].bitcast(FP4X4)
-                        lhs_s = (wb_s, wb_s_low)[a][:, c0:c0 + P]
-                        rhs_s = (v_s, v_s_low)[a][:, js]
+                        lhs_s = (wb_s, wb_s_pass1)[a][:, c0:c0 + P]
+                        rhs_s = (v_s, v_s_pass1)[a][:, js]
                     else:
-                        lhs = codes[(name, a, b)][:, t * P:(t + 1) * P].bitcast(FP8X4)
-                        lhs_s = scales[(name, a, b)][:, t * P:(t + 1) * P]
+                        lhs = codes[name, (a, b)][:, t * P:(t + 1) * P].bitcast(FP8X4)
+                        lhs_s = scales[name, (a, b)][:, t * P:(t + 1) * P]
                         rhs_s = v_s[4 * a:P, js]
                     nc.tensor.matmul_mx(out=bank[:, t, :], lhsT=lhs, lhsT_scale=lhs_s, rhs=v_w[a][:, js].bitcast(FP8X4),
                                         rhs_scale=rhs_s, start=(a == 0), stop=(a == PASSES - 1))
-            return bank.rearrange("p t n -> p n t")
+            return bank.rearrange("p t (n e) -> p n t e", e=2)
 
-        hb = [raw_tiles[3 * b][:].rearrange("p j c -> p (j c)").rearrange("p (n t) -> p n t", t=PACK) for b in range(PASSES)]
+        def rounded_columns(name, b, jq):
+            cols = rounded[name, b][:, jq * JQ * PACK:(jq + 1) * JQ * PACK]
+            return cols.rearrange("p (n e t) -> p n t e", t=PACK, e=2)
 
-        def pre_cols(key, jq):
-            return pre[slot[key]][:, jq * JQ * PACK:(jq + 1) * JQ * PACK].rearrange("p (n t) -> p n t", t=PACK)
+        def hb_columns(b, jq):
+            home = raw["wc", (chunks[0], chunks[-1])[b]]
+            return home[:, jq, :].rearrange("p (n t e) -> p n t e", t=PACK, e=2)
 
         def make_hb(b, jq):
-            nc.scalar.copy(out=hb[b][:, jq * JQ:(jq + 1) * JQ, :], in_=first_stage("wb", b, jq))
+            nc.scalar.copy(out=hb_columns(b, jq), in_=first_stage("wb", b, jq))
 
         def make_mild(b, jq):
-            nc.vector.tensor_tensor(pre_cols(("mild", b), jq), first_stage("wc", b, jq),
-                                    gain_t[:, b:b + 1, :].to_broadcast([P, JQ, PACK]), ALU.mult)
+            nc.vector.tensor_tensor(rounded_columns("mild", b, jq), first_stage("wc", b, jq),
+                                    gain_t[:, b:b + 1, :].unsqueeze(3).to_broadcast([P, JQ // 2, PACK, 2]), ALU.mult)
 
         def make_low(b, jq):
-            nc.vector.tensor_tensor(pre_cols(("low", b), jq), first_stage("wa", b, jq), hb[b][:, jq * JQ:(jq + 1) * JQ, :], ALU.min)
+            nc.vector.tensor_tensor(rounded_columns("low", b, jq), first_stage("wa", b, jq), hb_columns(b, jq), ALU.min)
+
+        def view_step(name, make, b, jq):
+            if jq == 0:
+                rounded_tile(name, b)
+            make(b, jq)
+            if jq == 0 and b > 0:
+                quantize(name, b - 1)
 
         def second_stage(name, u):
             bank = next_bank("scalar" if name == "mild" else "vector")
             ms = slice(u * P, (u + 1) * P)
             for b in range(PASSES):
                 nc.tensor.matmul_mx(out=bank[:], lhsT=v2_w[b][:, ms].bitcast(FP8X4), lhsT_scale=v2_s[4 * b:P, ms],
-                                    rhs=codes[(name, b)][:].bitcast(FP8X4), rhs_scale=scales[(name, b)][:],
+                                    rhs=codes[name, b][:].bitcast(FP8X4), rhs_scale=scales[name, b][:],
                                     start=(b == 0), stop=(b == PASSES - 1))
             return bank[:]
 
-        damp = [keep.tile([P, S], F32, name=f"damp{u}") for u in range(S2 // P)]
         mag = {}
+        damp = [keep.tile([P, S], F32, name=f"damp{u}") for u in range(TILES)]
 
         def make_mag(u):
-            mag[u] = ring.tile([P, S], F32, name=f"mag{u}", tag="mag")
+            mag[u] = steps.tile([P, S], F32, name=f"mag{u}", tag="mag")
             nc.scalar.activation(mag[u][:], second_stage("mild", u), ACT.Abs)
 
         def make_damp(u):
-            root = ring.tile([P, S], F32, name=f"root{u}", tag="root")
+            root = steps.tile([P, S], F32, name=f"root{u}", tag="root")
             nc.scalar.activation(root[:], mag[u][:], ACT.Abs_reciprocal_sqrt, bias=1.0)
-            if u in (2, 3, 4, 5):
+            if u in GPSIMD_SQUARES:
                 for c in range(0, S, S // 2):
                     nc.gpsimd.tensor_tensor(damp[u][:, c:c + S // 2], root[:, c:c + S // 2], root[:, c:c + S // 2], ALU.mult)
             else:
                 nc.scalar.activation(damp[u][:], root[:], ACT.Square)
 
-        def finish(u):
-            prod = ring.tile([P, S], F32, name=f"prod{u}", tag="prod")
+        def finish(u, base_t):
+            prod = steps.tile([P, S], F32, name=f"prod{u}", tag="prod")
             nc.vector.tensor_tensor(prod[:], second_stage("low", u), damp[u][:], ALU.mult)
             res = keep.tile([P, S], F32, name=f"res{u}")
-            if u < 6:
+            if u < TILES - SCALAR_BASE_TILES:
                 nc.gpsimd.tensor_scalar(res[:], prod[:], 1.0, base_t[:, u:u + 1], ALU.mult, ALU.add)
             else:
                 nc.scalar.activation(res[:], prod[:], ACT.Identity, bias=base_t[:, u:u + 1])
             nc.sync.dma_start(out=out[u * P:(u + 1) * P, :], in_=res[:])
 
-        def gather(dst, src, lst):
-            nc.vector.tensor_copy(dst[:], src.indirect(lst[:]))
+        for chunk in chunks:
+            round_weight("wc", chunk, shared=chunk[1] > 0)
+            quantize("wc", chunk)
+        for a in range(PASSES):
+            load_weight("wa", (a, 1), raw["wc", chunks[1 + a]])
+        for b in range(PASSES):
+            for jq in range(QUARTERS):
+                make_hb(b, jq)
+            for jq in range(QUARTERS):
+                view_step("mild", make_mild, b, jq)
+        quantize("mild", PASSES - 1)
 
-        def deal_wb_words():
-            nc.vector.tensor_copy(out=wb_w[:].rearrange("p a c -> p (a c)").bitcast(U16).rearrange("p (b t m) -> p b t m", t=PACK, m=P),
-                                  in_=wb_w_raw[:].rearrange("p a c -> p (a c)").bitcast(U16).rearrange("p (b m t) -> p b t m", t=PACK, m=P))
-
-        def deal_wb_scales():
-            nc.vector.tensor_copy(out=wb_s[:].rearrange("p (b t m) -> p b t m", b=2, t=PACK),
-                                  in_=wb_s_raw[:].rearrange("p (b m t) -> p b t m", b=2, t=PACK))
-
-        warm = keep.tile([P, 2], F32, name="warm")
-        nc.vector.memset(warm[:, 0:1], 1.0)
-        nc.scalar.activation(warm[:, 1:2], warm[:, 0:1], ACT.Abs_reciprocal_sqrt, bias=1.0)
-        nc.sync.dma_start(offs_t[:], offs)
-        nc.sync.dma_start(offs2_t[:], offs2)
-        tab_s_in = keep.tile([P, T], U8, name="tab_s_in", align_bytes=64)
-        for q in range(4): load_scales(nc.sync, tab_s_in, tab_scales, q)
-        nc.sync.dma_start(out=wb_w_raw[:].bitcast(I32), in_=wb_words.rearrange("a p c -> p a c").bitcast(I32))
-        load_tab()
-        for q in range(4): load_scales(nc.scalar, wb_s_raw, wb_scales, q)
-        load_w("wc", 0, 0)
-        nc.sync.dma_start(out=gain_t[:], in_=gain.rearrange("(b p t) -> p b t", p=P, t=PACK))
-        load_w("wc", 1, 0)
-        load_w("wc", 0, 1)
-        load_w("wc", 1, 1)
-        load_w("wa", 0, 0)
-        load_w("wa", 1, 0)
-        load_w("wa", 0, 1)
-        load_w("wa", 1, 1, 0, 1)
-        load_w("wa", 1, 1, 1, 2)
+        base_t = held([P, TILES], F32, "base_t", tag=f"scales_wc{len(chunks) - 1}")
         with nc.allow_non_contiguous_dma(reason="one base value for each partition and output tile"):
             nc.sync.dma_start(out=base_t[:], in_=base.rearrange("(u p) -> p u", p=P))
-        for q in range(4): nc.vector.tensor_copy(tab_s[32 * q:32 * q + 8, :].bitcast(I32), tab_s_in[32 * q:32 * q + 8, :].bitcast(I32))
-        gather(v_s, tab_s[:], offs_t)
-        shift_rows(nc.scalar, v_s_low, v_s)
-        deal_wb_words()
-        deal_wb_scales()
-        shift_rows(nc.scalar, wb_s_low, wb_s)
-        gather(v_w[0], tab_w[:, 0, :], offs_t)
-        gather(v_w[1], tab_w[:, 1, :], offs_t)
-        gather(v2_s, tab_s[:], offs2_t)
-        gather(v2_w[0], tab_w[:, 0, :], offs2_t)
-        gather(v2_w[1], tab_w[:, 1, :], offs2_t)
-        cast("wc", 0, 0, 0, "s")
-        cast("wc", 0, 0, 1, "g")
-        cast("wc", 1, 0, 0, "s")
-        cast("wc", 1, 0, 1, "g")
-        quant("wc", 0, 0)
-        quant("wc", 1, 0)
-        for jq in range(4): make_hb(0, jq)
-        cast("wc", 0, 1, 0, "s")
-        cast("wc", 0, 1, 1, "g")
-        cast("wc", 1, 1, 0, "s")
-        cast("wc", 1, 1, 1, "g")
-        make_mild(0, 0)
-        make_mild(0, 1)
-        quant("wc", 0, 1)
-        make_mild(0, 2)
-        quant("wc", 1, 1)
-        make_mild(0, 3)
-        for jq in range(4): make_hb(1, jq)
-        make_mild(1, 0)
-        quant("mild", 0)
-        make_mild(1, 1)
-        make_mild(1, 2)
-        make_mild(1, 3)
-        cast("wa", 0, 0, 0, "s")
-        cast("wa", 0, 0, 1, "g")
-        cast("wa", 1, 0, 0, "s")
-        cast("wa", 1, 0, 1, "g")
-        quant("wa", 0, 0)
-        quant("mild", 1)
-        make_mag(0)
-        make_mag(1)
-        cast("wa", 0, 1, 0, "g")
-        cast("wa", 0, 1, 1, "v")
-        quant("wa", 1, 0)
-        make_damp(0)
-        cast("wa", 1, 1, 0, "g")
-        make_low(0, 0)
-        cast("wa", 1, 1, 1, "v")
-        make_low(0, 1)
-        quant("wa", 0, 1)
-        make_mag(2)
-        make_damp(1)
-        make_low(0, 2)
-        quant("wa", 1, 1)
-        make_low(0, 3)
-        make_mag(3)
-        make_damp(2)
-        make_low(1, 0)
-        quant("low", 0)
-        make_low(1, 1)
-        make_mag(4)
-        make_damp(3)
-        make_low(1, 2)
-        make_low(1, 3)
-        make_mag(5)
-        make_damp(4)
-        quant("low", 1)
-        make_mag(6)
-        make_damp(5)
-        make_mag(7)
-        make_damp(6)
-        make_damp(7)
-        for u in range(8): finish(u)
+
+        for chunk in chunks:
+            round_weight("wa", chunk, shared=True)
+            quantize("wa", chunk)
+        for u in range(TILES):
+            make_mag(u)
+            view_step("low", make_low, *divmod(u, QUARTERS))
+            if u > 0:
+                make_damp(u - 1)
+        quantize("low", PASSES - 1)
+        make_damp(TILES - 1)
+
+        for u in range(TILES):
+            finish(u, base_t)

from contextlib import ExitStack

import concourse.mybir as mybir

K, T, S, S2 = 1024, 2048, 512, 1024
FLOPS = 2 * K * K * S * 3 + 2 * K * S2 * S * 2

F32 = mybir.dt.float32
BF16 = mybir.dt.bfloat16
I32 = mybir.dt.int32
U32 = mybir.dt.uint32
U16 = mybir.dt.uint16
U8 = mybir.dt.uint8
FP8X4 = mybir.dt.float8_e4m3fn_x4
FP4X4 = mybir.dt.float4_e2m1fn_x4
ALU = mybir.AluOpType
ACT = mybir.ActivationFunctionType

P = 128
PACK = 4
KP = P * PACK
PASSES = K // KP
QUADRANTS = 4
JQ = S // PACK
QUARTERS = S // JQ
TILES = S2 // P
assert TILES == PASSES * QUARTERS
READER_BANKS = 4
SHIFT_ROWS = 112
ROUNDED_TILES = 5
STEP_BUFS = 3
GPSIMD_SQUARES = range(3, 6)
SCALAR_BASE_TILES = 2


def tile_list_tank_mate_scores_kernel(tc, tab_words, tab_scales, offs, offs2, wa, wb_words, wb_scales, wc, gain, base, out):
    nc = tc.nc
    chunks = [(a, b) for b in range(PASSES) for a in range(PASSES)]
    with ExitStack() as ctx:
        keep = ctx.enter_context(tc.tile_pool(name="keep", bufs=1))
        steps = ctx.enter_context(tc.tile_pool(name="steps", bufs=STEP_BUFS))
        psum = ctx.enter_context(tc.psum_pool(name="psum", bufs=1))

        def held(shape, dtype, name, tag=None):
            return keep.tile(shape, dtype, name=name, tag=tag or name, align_bytes=64)

        banks = [psum.tile([P, S], F32, name=f"bank{i}") for i in range(2 * READER_BANKS)]
        taken = {"scalar": [], "vector": []}

        def next_bank(reader):
            first = 0 if reader == "scalar" else READER_BANKS
            taken[reader].append(banks[first + len(taken[reader]) % READER_BANKS])
            return taken[reader][-1]

        offs_t = keep.tile([P, S // 16], U16, name="offs_t")
        offs2_t = keep.tile([P, S2 // 16], U16, name="offs2_t")
        gain_t = keep.tile([P, PASSES, PACK], F32, name="gain_t")
        tab_s_in = held([P, T], U8, "tab_s_in")
        tab_s = held([P, T], U8, "tab_s")
        tab_w = held([P, PASSES, T], U32, "tab_w")
        wb_s_in = held([P, K], U8, "wb_s_in")
        wb_w_in = held([P, PASSES, 2 * K], U8, "wb_w_in")
        wb_s = held([P, K], U8, "wb_s")
        wb_w = held([P, PASSES, 2 * K], U8, "wb_w")
        v_s = held([P, S], U8, "v_s")
        v2_s = held([P, S2], U8, "v2_s")
        v_w = [held([P, S], U32, f"v_w{a}") for a in range(PASSES)]
        v2_w = [held([P, S2], U32, f"v2_w{a}") for a in range(PASSES)]
        v_s_pass1 = held([P, S], U8, "v_s_pass1")
        wb_s_pass1 = held([P, K], U8, "wb_s_pass1")

        def load_scales(dst, src):
            for q in range(QUADRANTS):
                nc.sync.dma_start(out=dst[32 * q:32 * q + 8, :].bitcast(I32), in_=src[:, 4 * q:4 * q + 4, :].bitcast(I32))

        def shift_down(dst, src):
            nc.sync.dma_start(out=dst[0:SHIFT_ROWS, :].bitcast(I32), in_=src[4:4 + SHIFT_ROWS, :].bitcast(I32))

        def gather(dst, window, offsets):
            nc.vector.tensor_copy(dst[:], window.indirect(offsets[:]))

        raw = {}

        def load_weight(name, chunk, home):
            a, b = chunk
            raw[name, chunk] = home
            w = wa if name == "wa" else wc
            nc.sync.dma_start(out=home, in_=w[a * KP:(a + 1) * KP, b * KP:(b + 1) * KP].rearrange("(p i) c -> p i c", i=PACK))

        nc.vector.memset(wb_s_in[:].bitcast(I32), 0)
        nc.vector.memset(tab_s[:].bitcast(I32), 0)
        nc.vector.memset(v_s_pass1[96:P, :].bitcast(I32), 0)
        nc.vector.memset(wb_s_pass1[96:P, :].bitcast(I32), 0)

        warm = keep.tile([P, 2], F32, name="warm")
        nc.vector.memset(warm[:, 0:1], 1.0)
        nc.scalar.activation(warm[:, 1:2], warm[:, 0:1], ACT.Abs_reciprocal_sqrt, bias=1.0)

        nc.sync.dma_start(offs_t[:], offs)
        nc.sync.dma_start(offs2_t[:], offs2)
        load_scales(tab_s_in, tab_scales)
        nc.sync.dma_start(out=wb_w_in[:].bitcast(I32), in_=wb_words.rearrange("a p c -> p a c").bitcast(I32))
        nc.sync.dma_start(out=gain_t[:], in_=gain.rearrange("(b p t) -> p b t", p=P, t=PACK))
        load_scales(wb_s_in, wb_scales)
        nc.sync.dma_start(out=tab_w[:].bitcast(I32), in_=tab_words.rearrange("a p t i -> p a (t i)").bitcast(I32))
        load_weight("wc", chunks[0], held([P, PACK, KP], F32, "raw_first")[:])

        for q in range(QUADRANTS):
            rows = slice(32 * q, 32 * q + 8)
            nc.vector.tensor_copy(tab_s[rows, :].bitcast(I32), tab_s_in[rows, :].bitcast(I32))
        gather(v_s, tab_s[:], offs_t)
        shift_down(v_s_pass1, v_s)
        nc.vector.tensor_copy(out=wb_s[:].rearrange("p (b t m) -> p b t m", t=PACK, m=P),
                              in_=wb_s_in[:].rearrange("p (b m t) -> p b t m", t=PACK, m=P))
        shift_down(wb_s_pass1, wb_s)
        nc.vector.tensor_copy(out=wb_w[:].rearrange("p a c -> p (a c)").bitcast(U16).rearrange("p (g t m) -> p g t m", t=PACK, m=P),
                              in_=wb_w_in[:].rearrange("p a c -> p (a c)").bitcast(U16).rearrange("p (g m t) -> p g t m", t=PACK, m=P))
        for a in range(PASSES):
            gather(v_w[a], tab_w[:, a, :], offs_t)
        gather(v2_s, tab_s[:], offs2_t)
        for a in range(PASSES):
            gather(v2_w[a], tab_w[:, a, :], offs2_t)

        load_weight("wc", chunks[1], held([P, PACK, KP], F32, "raw_second", tag="wb_s_in")[:])
        for name, b, tag in (("wc", 1, "wb_w_in"), ("wa", 0, "tab_s")):
            both = held([P, PASSES, PACK, KP], F32, f"raw_{name}{b}", tag=tag)
            for a in range(PASSES):
                load_weight(name, (a, b), both[:, a, :, :])

        rounded, codes, scales = {}, {}, {}

        def rounded_tile(name, key):
            n = len(rounded)
            rounded[name, key] = held([P, PACK * KP], BF16, f"rounded_{name}{n}", tag=f"rounded{n % ROUNDED_TILES}")

        def round_weight(name, chunk, shared):
            rounded_tile(name, chunk)
            dst = rounded[name, chunk][:].rearrange("p (t m i) -> p m i t", t=PACK, i=PACK)
            src = raw[name, chunk].rearrange("p i (m t) -> p m i t", t=PACK)
            for half in range(2):
                ts = slice(2 * half, 2 * half + 2)
                if half == 0 or not shared:
                    nc.scalar.copy(out=dst[:, :, :, ts], in_=src[:, :, :, ts])
                else:
                    nc.vector.tensor_copy(out=dst[:, :, :, ts], in_=src[:, :, :, ts])

        def quantize(name, key):
            codes[name, key] = held([P, KP], U32, f"codes_{name}{len(codes)}")
            scales[name, key] = held([P, KP], U8, f"scales_{name}{len(scales)}")
            nc.vector.quantize_mx(out=codes[name, key][:].bitcast(FP8X4), scales=scales[name, key][:], in_=rounded[name, key][:])

        def first_stage(name, b, jq):
            bank = next_bank("scalar" if name == "wb" else "vector")[:].rearrange("p (t n) -> p t n", t=PACK)
            js = slice(jq * JQ, (jq + 1) * JQ)
            for t in range(PACK):
                for a in range(PASSES):
                    if name == "wb":
                        c0 = b * KP + t * P
                        lhs = wb_w[:, a, 2 * c0:2 * (c0 + P)].bitcast(FP4X4)
                        lhs_s = (wb_s, wb_s_pass1)[a][:, c0:c0 + P]
                        rhs_s = (v_s, v_s_pass1)[a][:, js]
                    else:
                        lhs = codes[name, (a, b)][:, t * P:(t + 1) * P].bitcast(FP8X4)
                        lhs_s = scales[name, (a, b)][:, t * P:(t + 1) * P]
                        rhs_s = v_s[4 * a:P, js]
                    nc.tensor.matmul_mx(out=bank[:, t, :], lhsT=lhs, lhsT_scale=lhs_s, rhs=v_w[a][:, js].bitcast(FP8X4),
                                        rhs_scale=rhs_s, start=(a == 0), stop=(a == PASSES - 1))
            return bank.rearrange("p t (n e) -> p n t e", e=2)

        def rounded_columns(name, b, jq):
            cols = rounded[name, b][:, jq * JQ * PACK:(jq + 1) * JQ * PACK]
            return cols.rearrange("p (n e t) -> p n t e", t=PACK, e=2)

        def hb_columns(b, jq):
            home = raw["wc", (chunks[0], chunks[-1])[b]]
            return home[:, jq, :].rearrange("p (n t e) -> p n t e", t=PACK, e=2)

        def make_hb(b, jq):
            nc.scalar.copy(out=hb_columns(b, jq), in_=first_stage("wb", b, jq))

        def make_mild(b, jq):
            nc.vector.tensor_tensor(rounded_columns("mild", b, jq), first_stage("wc", b, jq),
                                    gain_t[:, b:b + 1, :].unsqueeze(3).to_broadcast([P, JQ // 2, PACK, 2]), ALU.mult)

        def make_low(b, jq):
            nc.vector.tensor_tensor(rounded_columns("low", b, jq), first_stage("wa", b, jq), hb_columns(b, jq), ALU.min)

        def view_step(name, make, b, jq):
            if jq == 0:
                rounded_tile(name, b)
            make(b, jq)
            if jq == 0 and b > 0:
                quantize(name, b - 1)

        def second_stage(name, u):
            bank = next_bank("scalar" if name == "mild" else "vector")
            ms = slice(u * P, (u + 1) * P)
            for b in range(PASSES):
                nc.tensor.matmul_mx(out=bank[:], lhsT=v2_w[b][:, ms].bitcast(FP8X4), lhsT_scale=v2_s[4 * b:P, ms],
                                    rhs=codes[name, b][:].bitcast(FP8X4), rhs_scale=scales[name, b][:],
                                    start=(b == 0), stop=(b == PASSES - 1))
            return bank[:]

        mag = {}
        damp = [keep.tile([P, S], F32, name=f"damp{u}") for u in range(TILES)]

        def make_mag(u):
            mag[u] = steps.tile([P, S], F32, name=f"mag{u}", tag="mag")
            nc.scalar.activation(mag[u][:], second_stage("mild", u), ACT.Abs)

        def make_damp(u):
            root = steps.tile([P, S], F32, name=f"root{u}", tag="root")
            nc.scalar.activation(root[:], mag[u][:], ACT.Abs_reciprocal_sqrt, bias=1.0)
            if u in GPSIMD_SQUARES:
                for c in range(0, S, S // 2):
                    nc.gpsimd.tensor_tensor(damp[u][:, c:c + S // 2], root[:, c:c + S // 2], root[:, c:c + S // 2], ALU.mult)
            else:
                nc.scalar.activation(damp[u][:], root[:], ACT.Square)

        def finish(u, base_t):
            prod = steps.tile([P, S], F32, name=f"prod{u}", tag="prod")
            nc.vector.tensor_tensor(prod[:], second_stage("low", u), damp[u][:], ALU.mult)
            res = keep.tile([P, S], F32, name=f"res{u}")
            if u < TILES - SCALAR_BASE_TILES:
                nc.gpsimd.tensor_scalar(res[:], prod[:], 1.0, base_t[:, u:u + 1], ALU.mult, ALU.add)
            else:
                nc.scalar.activation(res[:], prod[:], ACT.Identity, bias=base_t[:, u:u + 1])
            nc.sync.dma_start(out=out[u * P:(u + 1) * P, :], in_=res[:])

        for chunk in chunks:
            round_weight("wc", chunk, shared=chunk[1] > 0)
            quantize("wc", chunk)
        for a in range(PASSES):
            load_weight("wa", (a, 1), raw["wc", chunks[1 + a]])
        for b in range(PASSES):
            for jq in range(QUARTERS):
                make_hb(b, jq)
            for jq in range(QUARTERS):
                view_step("mild", make_mild, b, jq)
        quantize("mild", PASSES - 1)

        base_t = held([P, TILES], F32, "base_t", tag=f"scales_wc{len(chunks) - 1}")
        with nc.allow_non_contiguous_dma(reason="one base value for each partition and output tile"):
            nc.sync.dma_start(out=base_t[:], in_=base.rearrange("(u p) -> p u", p=P))

        for chunk in chunks:
            round_weight("wa", chunk, shared=True)
            quantize("wa", chunk)
        for u in range(TILES):
            make_mag(u)
            view_step("low", make_low, *divmod(u, QUARTERS))
            if u > 0:
                make_damp(u - 1)
        quantize("low", PASSES - 1)
        make_damp(TILES - 1)

        for u in range(TILES):
            finish(u, base_t)
